import numpy as np
import ml_dtypes

BF16 = ml_dtypes.bfloat16


def bf(x):
    return np.asarray(x, np.float32).astype(BF16)


def f32(x):
    return np.asarray(x, np.float32)


def f64(x):
    return np.asarray(x).astype(np.float64)


def striped(idx):
    return np.tile(idx.reshape(-1, 16).T, (8, 1))


def rows(idx, k):
    return np.tile(idx, (k, 1))


def look(tab, idx):
    return np.take_along_axis(f64(tab), rows(idx, len(tab)), axis=1)


K, S, V, N, M = 256, 2048, 1536, 1536, 512


def silu(v):
    return v / (1.0 + np.exp(-v))


def setup_inputs():
    return {"tab": bf(np.random.standard_normal((K, S))), "y": f32(np.random.standard_normal((K, V))), "w": bf(np.random.standard_normal((K, M)) / np.sqrt(K)), "offs": striped(np.random.permutation(S)[:N])}


def reference(tab, y, w, offs):
    idx = offs[:16].T.reshape(-1)
    t = look(tab, idx)
    x = silu(t) * f64(y)
    y = f64(w).T @ x
    return y

@@ -1,0 +1,64 @@
+import concourse.mybir as mybir
+
+P = 128
+R = 256
+S = 2048
+N = 1536
+M = 512
+PIECE = 512
+FLOPS = 2 * R * M * N
+
+BF16, F32, U16 = mybir.dt.bfloat16, mybir.dt.float32, mybir.dt.uint16
+SILU = mybir.ActivationFunctionType.Silu
+MULT = mybir.AluOpType.mult
+
+
+def tile_lookup_gate_silu_none_kernel(tc, tab, y, w, offs, out):
+    nc = tc.nc
+    row_blocks = R // P
+    out_blocks = M // P
+    pieces = N // PIECE
+    y_blocks = y.rearrange("(r p) n -> p r n", p=P)
+    w_blocks = w.rearrange("(r p) m -> p r m", p=P)
+
+    with (
+        tc.tile_pool(name="held", bufs=1) as held,
+        tc.tile_pool(name="work", bufs=2 * row_blocks) as work,
+        tc.tile_pool(name="staging", bufs=2 * out_blocks) as staging,
+        tc.psum_pool(name="psum", bufs=2 * out_blocks) as psum,
+    ):
+        offsets = held.tile([P, N // 16], U16, name="offsets")
+        nc.sync.dma_start(offsets[:], offs)
+        windows = []
+        for r in range(row_blocks):
+            window = held.tile([P, S], BF16, name=f"window{r}")
+            nc.sync.dma_start(window[:], tab[r * P : (r + 1) * P, :])
+            windows.append(window)
+        streams = [held.tile([P, row_blocks, PIECE], F32, name=f"stream{c}") for c in range(pieces)]
+        nc.sync.dma_start(streams[0][:], y_blocks[:, :, 0:PIECE])
+        weights = held.tile([P, row_blocks, M], BF16, name="weights")
+        nc.sync.dma_start(weights[:], w_blocks)
+        for c in range(1, pieces):
+            nc.sync.dma_start(streams[c][:], y_blocks[:, :, c * PIECE : (c + 1) * PIECE])
+
+        for c in range(pieces):
+            columns = slice(c * PIECE, (c + 1) * PIECE)
+            piece_offsets = offsets[:, c * PIECE // 16 : (c + 1) * PIECE // 16]
+            banks = [psum.tile([P, PIECE], F32, name=f"bank{c}_{m}", tag="bank") for m in range(out_blocks)]
+            for r in range(row_blocks):
+                gate = work.tile([P, PIECE], F32, name="gate")
+                nc.scalar.activation(gate[:], windows[r][:].indirect(piece_offsets), SILU)
+                x = work.tile([P, PIECE], BF16, name="x")
+                nc.vector.tensor_tensor(x[:], gate[:], streams[c][:, r, :], MULT)
+                for m in range(out_blocks):
+                    nc.tensor.matmul(
+                        banks[m][:],
+                        weights[:, r, m * P : (m + 1) * P],
+                        x[:],
+                        start=(r == 0),
+                        stop=(r == row_blocks - 1),
+                    )
+            for m in range(out_blocks):
+                staged = staging.tile([P, PIECE], F32, name="staged")
+                nc.vector.tensor_copy(staged[:], banks[m][:])
+                nc.sync.dma_start(out[m * P : (m + 1) * P, columns], staged[:])

@@ -27,6 +27,11 @@ def tile_lookup_gate_silu_none_kernel(tc, tab, y, w, offs, out):
         tc.tile_pool(name="staging", bufs=2 * out_blocks) as staging,
         tc.psum_pool(name="psum", bufs=2 * out_blocks) as psum,
     ):
+        zero = held.tile([P, 1], F32, name="zero")
+        nc.vector.memset(zero[:], 0.0)
+        silu_of_zero = held.tile([P, 1], F32, name="silu_of_zero")
+        nc.scalar.activation(silu_of_zero[:], zero[:], SILU)
+
         offsets = held.tile([P, N // 16], U16, name="offsets")
         nc.sync.dma_start(offsets[:], offs)
         windows = []

@@ -18,13 +18,12 @@ def tile_lookup_gate_silu_none_kernel(tc, tab, y, w, offs, out):
     row_blocks = R // P
     out_blocks = M // P
     pieces = N // PIECE
-    y_blocks = y.rearrange("(r p) n -> p r n", p=P)
     w_blocks = w.rearrange("(r p) m -> p r m", p=P)
 
     with (
         tc.tile_pool(name="held", bufs=1) as held,
-        tc.tile_pool(name="work", bufs=2 * row_blocks) as work,
-        tc.tile_pool(name="staging", bufs=2 * out_blocks) as staging,
+        tc.tile_pool(name="work", bufs=(N // PIECE) * row_blocks) as work,
+        tc.tile_pool(name="staging", bufs=3 * out_blocks) as staging,
         tc.psum_pool(name="psum", bufs=2 * out_blocks) as psum,
     ):
         zero = held.tile([P, 1], F32, name="zero")
@@ -39,31 +38,50 @@ def tile_lookup_gate_silu_none_kernel(tc, tab, y, w, offs, out):
             window = held.tile([P, S], BF16, name=f"window{r}")
             nc.sync.dma_start(window[:], tab[r * P : (r + 1) * P, :])
             windows.append(window)
-        streams = [held.tile([P, row_blocks, PIECE], F32, name=f"stream{c}") for c in range(pieces)]
-        nc.sync.dma_start(streams[0][:], y_blocks[:, :, 0:PIECE])
+        streams = {}
         weights = held.tile([P, row_blocks, M], BF16, name="weights")
-        nc.sync.dma_start(weights[:], w_blocks)
-        for c in range(1, pieces):
-            nc.sync.dma_start(streams[c][:], y_blocks[:, :, c * PIECE : (c + 1) * PIECE])
-
         for c in range(pieces):
-            columns = slice(c * PIECE, (c + 1) * PIECE)
+            for r in range(row_blocks):
+                stream = held.tile([P, PIECE], F32, name=f"stream{c}_{r}")
+                nc.sync.dma_start(stream[:], y[r * P : (r + 1) * P, c * PIECE : (c + 1) * PIECE])
+                streams[c, r] = stream
+                if c == 0 and r == 0:
+                    nc.sync.dma_start(weights[:], w_blocks)
+
+        gates = {}
+        for c in range(pieces):
             piece_offsets = offsets[:, c * PIECE // 16 : (c + 1) * PIECE // 16]
-            banks = [psum.tile([P, PIECE], F32, name=f"bank{c}_{m}", tag="bank") for m in range(out_blocks)]
             for r in range(row_blocks):
                 gate = work.tile([P, PIECE], F32, name="gate")
                 nc.scalar.activation(gate[:], windows[r][:].indirect(piece_offsets), SILU)
-                x = work.tile([P, PIECE], BF16, name="x")
-                nc.vector.tensor_tensor(x[:], gate[:], streams[c][:, r, :], MULT)
-                for m in range(out_blocks):
-                    nc.tensor.matmul(
-                        banks[m][:],
-                        weights[:, r, m * P : (m + 1) * P],
-                        x[:],
-                        start=(r == 0),
-                        stop=(r == row_blocks - 1),
-                    )
+                gates[c, r] = gate
+
+        banks = {}
+
+        def multiply(c, r):
+            x = work.tile([P, PIECE], BF16, name="x")
+            nc.vector.tensor_tensor(x[:], gates[c, r][:], streams[c, r][:], MULT)
             for m in range(out_blocks):
+                if r == 0:
+                    banks[c, m] = psum.tile([P, PIECE], F32, name=f"bank{c}_{m}", tag="bank")
+                nc.tensor.matmul(
+                    banks[c, m][:],
+                    weights[:, r, m * P : (m + 1) * P],
+                    x[:],
+                    start=(r == 0),
+                    stop=(r == row_blocks - 1),
+                )
+
+        copies_a_multiply = out_blocks // row_blocks
+        for r in range(row_blocks):
+            multiply(0, r)
+        for c in range(pieces):
+            for m in range(out_blocks):
+                if c + 1 < pieces and m % copies_a_multiply == 0:
+                    multiply(c + 1, m // copies_a_multiply)
                 staged = staging.tile([P, PIECE], F32, name="staged")
-                nc.vector.tensor_copy(staged[:], banks[m][:])
-                nc.sync.dma_start(out[m * P : (m + 1) * P, columns], staged[:])
+                if c > 0 and m % 2 == 1:
+                    nc.scalar.copy(staged[:], banks[c, m][:])
+                else:
+                    nc.vector.tensor_copy(staged[:], banks[c, m][:])
+                nc.sync.dma_start(out[m * P : (m + 1) * P, c * PIECE : (c + 1) * PIECE], staged[:])

@@ -6,6 +6,7 @@ S = 2048
 N = 1536
 M = 512
 PIECE = 512
+WARM_UPS = 8
 FLOPS = 2 * R * M * N
 
 BF16, F32, U16 = mybir.dt.bfloat16, mybir.dt.float32, mybir.dt.uint16
@@ -30,6 +31,12 @@ def tile_lookup_gate_silu_none_kernel(tc, tab, y, w, offs, out):
         nc.vector.memset(zero[:], 0.0)
         silu_of_zero = held.tile([P, 1], F32, name="silu_of_zero")
         nc.scalar.activation(silu_of_zero[:], zero[:], SILU)
+
+        zeros = held.tile([P, PIECE], BF16, name="zeros")
+        nc.gpsimd.memset(zeros[:], 0.0)
+        warm_bank = psum.tile([P, PIECE], F32, name="warm_bank", tag="bank")
+        for i in range(WARM_UPS):
+            nc.tensor.matmul(warm_bank[:], zeros[:, 0:P], zeros[:], start=True, stop=True)
 
         offsets = held.tile([P, N // 16], U16, name="offsets")
         nc.sync.dma_start(offsets[:], offs)

import concourse.mybir as mybir

P = 128
R = 256
S = 2048
N = 1536
M = 512
PIECE = 512
WARM_UPS = 8
FLOPS = 2 * R * M * N

BF16, F32, U16 = mybir.dt.bfloat16, mybir.dt.float32, mybir.dt.uint16
SILU = mybir.ActivationFunctionType.Silu
MULT = mybir.AluOpType.mult


def tile_lookup_gate_silu_none_kernel(tc, tab, y, w, offs, out):
    nc = tc.nc
    row_blocks = R // P
    out_blocks = M // P
    pieces = N // PIECE
    w_blocks = w.rearrange("(r p) m -> p r m", p=P)

    with (
        tc.tile_pool(name="held", bufs=1) as held,
        tc.tile_pool(name="work", bufs=(N // PIECE) * row_blocks) as work,
        tc.tile_pool(name="staging", bufs=3 * out_blocks) as staging,
        tc.psum_pool(name="psum", bufs=2 * out_blocks) as psum,
    ):
        zero = held.tile([P, 1], F32, name="zero")
        nc.vector.memset(zero[:], 0.0)
        silu_of_zero = held.tile([P, 1], F32, name="silu_of_zero")
        nc.scalar.activation(silu_of_zero[:], zero[:], SILU)

        zeros = held.tile([P, PIECE], BF16, name="zeros")
        nc.gpsimd.memset(zeros[:], 0.0)
        warm_bank = psum.tile([P, PIECE], F32, name="warm_bank", tag="bank")
        for i in range(WARM_UPS):
            nc.tensor.matmul(warm_bank[:], zeros[:, 0:P], zeros[:], start=True, stop=True)

        offsets = held.tile([P, N // 16], U16, name="offsets")
        nc.sync.dma_start(offsets[:], offs)
        windows = []
        for r in range(row_blocks):
            window = held.tile([P, S], BF16, name=f"window{r}")
            nc.sync.dma_start(window[:], tab[r * P : (r + 1) * P, :])
            windows.append(window)
        streams = {}
        weights = held.tile([P, row_blocks, M], BF16, name="weights")
        for c in range(pieces):
            for r in range(row_blocks):
                stream = held.tile([P, PIECE], F32, name=f"stream{c}_{r}")
                nc.sync.dma_start(stream[:], y[r * P : (r + 1) * P, c * PIECE : (c + 1) * PIECE])
                streams[c, r] = stream
                if c == 0 and r == 0:
                    nc.sync.dma_start(weights[:], w_blocks)

        gates = {}
        for c in range(pieces):
            piece_offsets = offsets[:, c * PIECE // 16 : (c + 1) * PIECE // 16]
            for r in range(row_blocks):
                gate = work.tile([P, PIECE], F32, name="gate")
                nc.scalar.activation(gate[:], windows[r][:].indirect(piece_offsets), SILU)
                gates[c, r] = gate

        banks = {}

        def multiply(c, r):
            x = work.tile([P, PIECE], BF16, name="x")
            nc.vector.tensor_tensor(x[:], gates[c, r][:], streams[c, r][:], MULT)
            for m in range(out_blocks):
                if r == 0:
                    banks[c, m] = psum.tile([P, PIECE], F32, name=f"bank{c}_{m}", tag="bank")
                nc.tensor.matmul(
                    banks[c, m][:],
                    weights[:, r, m * P : (m + 1) * P],
                    x[:],
                    start=(r == 0),
                    stop=(r == row_blocks - 1),
                )

        copies_a_multiply = out_blocks // row_blocks
        for r in range(row_blocks):
            multiply(0, r)
        for c in range(pieces):
            for m in range(out_blocks):
                if c + 1 < pieces and m % copies_a_multiply == 0:
                    multiply(c + 1, m // copies_a_multiply)
                staged = staging.tile([P, PIECE], F32, name="staged")
                if c > 0 and m % 2 == 1:
                    nc.scalar.copy(staged[:], banks[c, m][:])
                else:
                    nc.vector.tensor_copy(staged[:], banks[c, m][:])
                nc.sync.dma_start(out[m * P : (m + 1) * P, c * PIECE : (c + 1) * PIECE], staged[:])
